import numpy as np, ml_dtypes
CORES = [51,54,179,182]
N = 4
import mx_ref
NC = 512
BF = ml_dtypes.bfloat16
def setup_inputs(rng):
    def f(*shape):
        return mx_ref.flush((rng.standard_normal(shape, dtype=np.float32) * np.exp2(rng.integers(-2, 3, shape[:-1] + (1,)))).astype(BF))
    return {"w": f(N, 128, 512), "x": f(N, 128, 4 * NC)}
def setup_inputs_blocks(rng):
    d = setup_inputs(rng)
    for k in ("w", "x"): d[k] = mx_ref.spread(d[k], rng, 4)
    return d
def setup_inputs_wide(rng):
    d = setup_inputs(rng)
    for k in ("w", "x"): d[k] = mx_ref.flush((d[k].astype(np.float32) * np.exp2(rng.integers(-8, 9, (N, 1, 1))).astype(np.float32)).astype(BF))
    return d
def setup_inputs_zeros(rng):
    d = setup_inputs(rng); v = d["x"].reshape(N, 128, -1, 4).copy()
    v[np.broadcast_to((rng.random((N, 1, v.shape[2], 1)) < 0.33), v.shape)] = 0
    d["x"] = v.reshape(d["x"].shape)
    return d
def reference(w, x):
    QX = [mx_ref.quantize(x[j]) for j in range(N)]
    y = np.zeros((N, 128, NC), np.float32)
    for r in range(N):
        qw = mx_ref.quantize(w[r])
        for j in range(N):
            p = mx_ref.matmul(qw, QX[j])
            y[r] = p if j == 0 else np.maximum(y[r], p)
    return {"y": y}

@@ -1,0 +1,157 @@
+from concourse.bass import DstId, RemoteDMATransfer
+from concourse.mybir import dt, AluOpType
+
+N = 4
+NC = 512
+BANK = 512
+NBANKS = 8
+
+QCH = [(0, 256), (256, 512)]
+MCH = [(0, 256), (256, 512)]
+PIECES = [("c", 0, 256, True), ("s", 0, 512, False), ("c", 256, 512, False)]
+ORDER = [("me", 0), ("me", 1), ("near", 0), ("twin", 0), ("near", 1), ("cross", 0), ("twin", 1), ("cross", 1)]
+
+SCRATCH = {
+    "xb": ("sbuf", [128, 4 * NC], "bfloat16"),
+    "wb": ("sbuf", [128, 512], "bfloat16"),
+    "qw": ("sbuf", [128, 128], "float8_e4m3fn_x4"),
+    "sw": ("sbuf", [128, 128], "uint8"),
+    "qx": ("sbuf", [128, N * NC], "float8_e4m3fn_x4"),
+    "sx": ("sbuf", [128, N * NC], "uint8"),
+    "acc": ("sbuf", [128, NC], "float32"),
+    "ps": ("psum", [128, NBANKS * BANK], "float32"),
+}
+SEMAPHORES = (["ldw", "qw", "sent"]
+              + ["ldx%d" % i for i in range(len(QCH))]
+              + ["q%d" % i for i in range(len(QCH))]
+              + ["a%d_%d" % (j, p) for j in range(N) for p in range(len(PIECES))]
+              + ["m%d" % i for i in range(len(ORDER))]
+              + ["v%d" % i for i in range(len(MCH))]
+              + ["st%d" % i for i in range(len(MCH))])
+
+
+def _count(mask):
+    return bin(mask).count("1")
+
+
+def _meet(a, b, c, d):
+    return a < d and c < b
+
+
+def _wiring(c, T, topo):
+    w = {"me": c}
+    for o in T.cores:
+        if o == c:
+            continue
+        if topo.host(o) == topo.host(c) and topo.chip(o) == topo.chip(c):
+            w["near"] = o
+        elif topo.die(o) == topo.die(c):
+            w["twin"] = o
+        else:
+            w["cross"] = o
+    w["out"] = topo.mask(c, w["twin"]) & topo.mask(c, w["cross"])
+    w["stay"] = topo.mask(c, w["near"]) & ~w["out"]
+    return w
+
+
+def rank_program(g, core, T, topo):
+    me = T.rank_of(core)
+    if me is None:
+        return
+    W = _wiring(core, T, topo)
+    near, twin, cross = W["near"], W["twin"], W["cross"]
+
+    def view(kind, slot, a, b):
+        if kind == "c":
+            return T.qx[:, slot * NC + a:slot * NC + b].bitcast(dt.uint8)
+        return T.sx[:, slot * NC + a:slot * NC + b]
+
+    def dst(d):
+        rid, pid = topo.addr(d, core)
+        return DstId(rid=rid, pnc=pid)
+
+    for i, (a, b) in enumerate(QCH):
+        m = 2 * (a + b)
+        g.sync.dma_start(T.xb[:, 4 * a:m], T.x[:, 4 * a:m]).then_inc(T.sem["ldx%d" % i], 16)
+        g.scalar.dma_start(T.xb[:, m:4 * b], T.x[:, m:4 * b]).then_inc(T.sem["ldx%d" % i], 16)
+    g.sync.dma_start(T.wb[:], T.w[:]).then_inc(T.sem.ldw, 16)
+
+    for i, (a, b) in enumerate(QCH):
+        g.vector.wait_ge(T.sem["ldx%d" % i], 32)
+        g.vector.quantize_mx(T.qx[:, me * NC + a:me * NC + b], T.sx[:, me * NC + a:me * NC + b],
+                             T.xb[:, 4 * a:4 * b]).then_inc(T.sem["q%d" % i], 1)
+    g.vector.wait_ge(T.sem.ldw, 16)
+    g.vector.quantize_mx(T.qw[:], T.sw[:], T.wb[:]).then_inc(T.sem.qw, 1)
+
+    sent = 0
+    seen = set()
+    for p, (kind, a, b, relay) in enumerate(PIECES):
+        for i, (qa, qb) in enumerate(QCH):
+            if _meet(a, b, qa, qb) and i not in seen:
+                seen.add(i)
+                g.wait_ge(T.sem["q%d" % i], 1)
+        sem = T.sem["a%d_%d" % (me, p)]
+        fars = [twin] if relay else [twin, cross]
+        g.remote_dma_fused([
+            RemoteDMATransfer(dst_ids=[dst(d) for d in fars], dma_engine_mask=W["out"], remote_sem=sem,
+                              srcs=[view(kind, me, a, b)], dsts=[view(kind, me, a, b) for d in fars]),
+            RemoteDMATransfer(dst_ids=[dst(near)], dma_engine_mask=W["stay"], remote_sem=sem,
+                              srcs=[view(kind, me, a, b)], dsts=[view(kind, me, a, b)]),
+        ], local_sem=T.sem.sent)
+        sent += _count(W["out"]) + _count(W["stay"])
+
+    tw = T.rank_of(twin)
+    for p, (kind, a, b, relay) in enumerate(PIECES):
+        if not relay:
+            continue
+        sem = T.sem["a%d_%d" % (tw, p)]
+        g.wait_ge(sem, _count(_wiring(twin, T, topo)["out"]))
+        rid, pid = topo.addr(near, core)
+        g.remote_dma(view(kind, tw, a, b), view(kind, tw, a, b), sem, T.sem.sent, pid, rid, W["stay"])
+        sent += _count(W["stay"])
+
+    def landed(role, p):
+        src = _wiring(W[role], T, topo)
+        if role == "near":
+            return _count(src["stay"])
+        if role == "cross" and PIECES[p][3]:
+            return _count(_wiring(near, T, topo)["stay"])
+        return _count(src["out"])
+
+    g.tensor.wait_ge(T.sem.qw, 1)
+    done = [0] * len(MCH)
+    used = []
+    for k, (role, c) in enumerate(ORDER):
+        a, b = MCH[c]
+        j = T.rank_of(W[role])
+        if role == "me":
+            for i, (qa, qb) in enumerate(QCH):
+                if _meet(a, b, qa, qb):
+                    g.tensor.wait_ge(T.sem["q%d" % i], 1)
+        else:
+            for p, (kind, pa, pb, relay) in enumerate(PIECES):
+                if _meet(a, b, pa, pb):
+                    g.tensor.wait_ge(T.sem["a%d_%d" % (j, p)], landed(role, p))
+        if k >= NBANKS:
+            oc, on = used[k - NBANKS]
+            g.tensor.wait_ge(T.sem["v%d" % oc], on)
+        bank = (k % NBANKS) * BANK
+        prod = T.ps[:, bank:bank + (b - a)]
+        g.tensor.matmul_mx(prod, T.qw[:], T.sw[:], T.qx[:, j * NC + a:j * NC + b], T.sx[:, j * NC + a:j * NC + b],
+                           True, True).then_inc(T.sem["m%d" % k], 1)
+        g.vector.wait_ge(T.sem["m%d" % k], 1)
+        if done[c] == 0:
+            g.vector.tensor_copy(T.acc[:, a:b], prod).then_inc(T.sem["v%d" % c], 1)
+        else:
+            g.vector.wait_ge(T.sem["v%d" % c], done[c])
+            g.vector.tensor_tensor(T.acc[:, a:b], prod, T.acc[:, a:b], AluOpType.max).then_inc(T.sem["v%d" % c], 1)
+        done[c] += 1
+        used.append((c, done[c]))
+
+    for c, (a, b) in enumerate(MCH):
+        q = g.sync if c % 2 == 0 else g.scalar
+        q.wait_ge(T.sem["v%d" % c], N)
+        q.dma_start(T.y[:, a:b], T.acc[:, a:b]).then_inc(T.sem["st%d" % c], 16)
+        q.wait_ge(T.sem["st%d" % c], 16)
+
+    g.wait_ge(T.sem.sent, sent)

@@ -6,10 +6,11 @@ NC = 512
 BANK = 512
 NBANKS = 8
 
-QCH = [(0, 256), (256, 512)]
-MCH = [(0, 256), (256, 512)]
-PIECES = [("c", 0, 256, True), ("s", 0, 512, False), ("c", 256, 512, False)]
-ORDER = [("me", 0), ("me", 1), ("near", 0), ("twin", 0), ("near", 1), ("cross", 0), ("twin", 1), ("cross", 1)]
+QCH = [(0, 128), (128, 384), (384, 512)]
+MCH = [(0, 128), (128, 384), (384, 512)]
+PIECES = [("c", 0, 128, "stay"), ("c", 128, 384, "stay"), ("s", 0, 512, "stay"), ("c", 384, 512, None)]
+ORDER = [("me", 0), ("me", 1), ("me", 2), ("near", 0), ("near", 1), ("near", 2),
+         ("twin", 0), ("twin", 1), ("cross", 0), ("cross", 1), ("twin", 2), ("cross", 2)]
 
 SCRATCH = {
     "xb": ("sbuf", [128, 4 * NC], "bfloat16"),
@@ -50,7 +51,8 @@ def _wiring(c, T, topo):
         else:
             w["cross"] = o
     w["out"] = topo.mask(c, w["twin"]) & topo.mask(c, w["cross"])
-    w["stay"] = topo.mask(c, w["near"]) & ~w["out"]
+    w["all"] = topo.mask(c, w["near"])
+    w["stay"] = w["all"] & ~w["out"]
     return w
 
 
@@ -71,9 +73,8 @@ def rank_program(g, core, T, topo):
         return DstId(rid=rid, pnc=pid)
 
     for i, (a, b) in enumerate(QCH):
-        m = 2 * (a + b)
-        g.sync.dma_start(T.xb[:, 4 * a:m], T.x[:, 4 * a:m]).then_inc(T.sem["ldx%d" % i], 16)
-        g.scalar.dma_start(T.xb[:, m:4 * b], T.x[:, m:4 * b]).then_inc(T.sem["ldx%d" % i], 16)
+        g.sync.dma_start(T.xb[0:64, 4 * a:4 * b], T.x[0:64, 4 * a:4 * b]).then_inc(T.sem["ldx%d" % i], 16)
+        g.scalar.dma_start(T.xb[64:128, 4 * a:4 * b], T.x[64:128, 4 * a:4 * b]).then_inc(T.sem["ldx%d" % i], 16)
     g.sync.dma_start(T.wb[:], T.w[:]).then_inc(T.sem.ldw, 16)
 
     for i, (a, b) in enumerate(QCH):
@@ -85,13 +86,13 @@ def rank_program(g, core, T, topo):
 
     sent = 0
     seen = set()
-    for p, (kind, a, b, relay) in enumerate(PIECES):
+    for p, (kind, a, b, fwd) in enumerate(PIECES):
         for i, (qa, qb) in enumerate(QCH):
             if _meet(a, b, qa, qb) and i not in seen:
                 seen.add(i)
                 g.wait_ge(T.sem["q%d" % i], 1)
         sem = T.sem["a%d_%d" % (me, p)]
-        fars = [twin] if relay else [twin, cross]
+        fars = [twin] if fwd else [twin, cross]
         g.remote_dma_fused([
             RemoteDMATransfer(dst_ids=[dst(d) for d in fars], dma_engine_mask=W["out"], remote_sem=sem,
                               srcs=[view(kind, me, a, b)], dsts=[view(kind, me, a, b) for d in fars]),
@@ -101,22 +102,21 @@ def rank_program(g, core, T, topo):
         sent += _count(W["out"]) + _count(W["stay"])
 
     tw = T.rank_of(twin)
-    for p, (kind, a, b, relay) in enumerate(PIECES):
-        if not relay:
+    for p, (kind, a, b, fwd) in enumerate(PIECES):
+        if not fwd:
             continue
         sem = T.sem["a%d_%d" % (tw, p)]
         g.wait_ge(sem, _count(_wiring(twin, T, topo)["out"]))
         rid, pid = topo.addr(near, core)
-        g.remote_dma(view(kind, tw, a, b), view(kind, tw, a, b), sem, T.sem.sent, pid, rid, W["stay"])
-        sent += _count(W["stay"])
+        g.remote_dma(view(kind, tw, a, b), view(kind, tw, a, b), sem, T.sem.sent, pid, rid, W[fwd])
+        sent += _count(W[fwd])
 
     def landed(role, p):
-        src = _wiring(W[role], T, topo)
         if role == "near":
-            return _count(src["stay"])
-        if role == "cross" and PIECES[p][3]:
             return _count(_wiring(near, T, topo)["stay"])
-        return _count(src["out"])
+        if role == "cross" and PIECES[p][3]:
+            return _count(_wiring(near, T, topo)[PIECES[p][3]])
+        return _count(_wiring(W[role], T, topo)["out"])
 
     g.tensor.wait_ge(T.sem.qw, 1)
     done = [0] * len(MCH)
@@ -129,7 +129,7 @@ def rank_program(g, core, T, topo):
                 if _meet(a, b, qa, qb):
                     g.tensor.wait_ge(T.sem["q%d" % i], 1)
         else:
-            for p, (kind, pa, pb, relay) in enumerate(PIECES):
+            for p, (kind, pa, pb, fwd) in enumerate(PIECES):
                 if _meet(a, b, pa, pb):
                     g.tensor.wait_ge(T.sem["a%d_%d" % (j, p)], landed(role, p))
         if k >= NBANKS:
@@ -152,6 +152,8 @@ def rank_program(g, core, T, topo):
         q = g.sync if c % 2 == 0 else g.scalar
         q.wait_ge(T.sem["v%d" % c], N)
         q.dma_start(T.y[:, a:b], T.acc[:, a:b]).then_inc(T.sem["st%d" % c], 16)
+    for c in range(len(MCH)):
+        q = g.sync if c % 2 == 0 else g.scalar
         q.wait_ge(T.sem["st%d" % c], 16)
 
     g.wait_ge(T.sem.sent, sent)

from concourse.bass import DstId, RemoteDMATransfer
from concourse.mybir import dt, AluOpType

N = 4
NC = 512
BANK = 512
NBANKS = 8

QCH = [(0, 128), (128, 384), (384, 512)]
MCH = [(0, 128), (128, 384), (384, 512)]
PIECES = [("c", 0, 128, "stay"), ("c", 128, 384, "stay"), ("s", 0, 512, "stay"), ("c", 384, 512, None)]
ORDER = [("me", 0), ("me", 1), ("me", 2), ("near", 0), ("near", 1), ("near", 2),
         ("twin", 0), ("twin", 1), ("cross", 0), ("cross", 1), ("twin", 2), ("cross", 2)]

SCRATCH = {
    "xb": ("sbuf", [128, 4 * NC], "bfloat16"),
    "wb": ("sbuf", [128, 512], "bfloat16"),
    "qw": ("sbuf", [128, 128], "float8_e4m3fn_x4"),
    "sw": ("sbuf", [128, 128], "uint8"),
    "qx": ("sbuf", [128, N * NC], "float8_e4m3fn_x4"),
    "sx": ("sbuf", [128, N * NC], "uint8"),
    "acc": ("sbuf", [128, NC], "float32"),
    "ps": ("psum", [128, NBANKS * BANK], "float32"),
}
SEMAPHORES = (["ldw", "qw", "sent"]
              + ["ldx%d" % i for i in range(len(QCH))]
              + ["q%d" % i for i in range(len(QCH))]
              + ["a%d_%d" % (j, p) for j in range(N) for p in range(len(PIECES))]
              + ["m%d" % i for i in range(len(ORDER))]
              + ["v%d" % i for i in range(len(MCH))]
              + ["st%d" % i for i in range(len(MCH))])


def _count(mask):
    return bin(mask).count("1")


def _meet(a, b, c, d):
    return a < d and c < b


def _wiring(c, T, topo):
    w = {"me": c}
    for o in T.cores:
        if o == c:
            continue
        if topo.host(o) == topo.host(c) and topo.chip(o) == topo.chip(c):
            w["near"] = o
        elif topo.die(o) == topo.die(c):
            w["twin"] = o
        else:
            w["cross"] = o
    w["out"] = topo.mask(c, w["twin"]) & topo.mask(c, w["cross"])
    w["all"] = topo.mask(c, w["near"])
    w["stay"] = w["all"] & ~w["out"]
    return w


def rank_program(g, core, T, topo):
    me = T.rank_of(core)
    if me is None:
        return
    W = _wiring(core, T, topo)
    near, twin, cross = W["near"], W["twin"], W["cross"]

    def view(kind, slot, a, b):
        if kind == "c":
            return T.qx[:, slot * NC + a:slot * NC + b].bitcast(dt.uint8)
        return T.sx[:, slot * NC + a:slot * NC + b]

    def dst(d):
        rid, pid = topo.addr(d, core)
        return DstId(rid=rid, pnc=pid)

    for i, (a, b) in enumerate(QCH):
        g.sync.dma_start(T.xb[0:64, 4 * a:4 * b], T.x[0:64, 4 * a:4 * b]).then_inc(T.sem["ldx%d" % i], 16)
        g.scalar.dma_start(T.xb[64:128, 4 * a:4 * b], T.x[64:128, 4 * a:4 * b]).then_inc(T.sem["ldx%d" % i], 16)
    g.sync.dma_start(T.wb[:], T.w[:]).then_inc(T.sem.ldw, 16)

    for i, (a, b) in enumerate(QCH):
        g.vector.wait_ge(T.sem["ldx%d" % i], 32)
        g.vector.quantize_mx(T.qx[:, me * NC + a:me * NC + b], T.sx[:, me * NC + a:me * NC + b],
                             T.xb[:, 4 * a:4 * b]).then_inc(T.sem["q%d" % i], 1)
    g.vector.wait_ge(T.sem.ldw, 16)
    g.vector.quantize_mx(T.qw[:], T.sw[:], T.wb[:]).then_inc(T.sem.qw, 1)

    sent = 0
    seen = set()
    for p, (kind, a, b, fwd) in enumerate(PIECES):
        for i, (qa, qb) in enumerate(QCH):
            if _meet(a, b, qa, qb) and i not in seen:
                seen.add(i)
                g.wait_ge(T.sem["q%d" % i], 1)
        sem = T.sem["a%d_%d" % (me, p)]
        fars = [twin] if fwd else [twin, cross]
        g.remote_dma_fused([
            RemoteDMATransfer(dst_ids=[dst(d) for d in fars], dma_engine_mask=W["out"], remote_sem=sem,
                              srcs=[view(kind, me, a, b)], dsts=[view(kind, me, a, b) for d in fars]),
            RemoteDMATransfer(dst_ids=[dst(near)], dma_engine_mask=W["stay"], remote_sem=sem,
                              srcs=[view(kind, me, a, b)], dsts=[view(kind, me, a, b)]),
        ], local_sem=T.sem.sent)
        sent += _count(W["out"]) + _count(W["stay"])

    tw = T.rank_of(twin)
    for p, (kind, a, b, fwd) in enumerate(PIECES):
        if not fwd:
            continue
        sem = T.sem["a%d_%d" % (tw, p)]
        g.wait_ge(sem, _count(_wiring(twin, T, topo)["out"]))
        rid, pid = topo.addr(near, core)
        g.remote_dma(view(kind, tw, a, b), view(kind, tw, a, b), sem, T.sem.sent, pid, rid, W[fwd])
        sent += _count(W[fwd])

    def landed(role, p):
        if role == "near":
            return _count(_wiring(near, T, topo)["stay"])
        if role == "cross" and PIECES[p][3]:
            return _count(_wiring(near, T, topo)[PIECES[p][3]])
        return _count(_wiring(W[role], T, topo)["out"])

    g.tensor.wait_ge(T.sem.qw, 1)
    done = [0] * len(MCH)
    used = []
    for k, (role, c) in enumerate(ORDER):
        a, b = MCH[c]
        j = T.rank_of(W[role])
        if role == "me":
            for i, (qa, qb) in enumerate(QCH):
                if _meet(a, b, qa, qb):
                    g.tensor.wait_ge(T.sem["q%d" % i], 1)
        else:
            for p, (kind, pa, pb, fwd) in enumerate(PIECES):
                if _meet(a, b, pa, pb):
                    g.tensor.wait_ge(T.sem["a%d_%d" % (j, p)], landed(role, p))
        if k >= NBANKS:
            oc, on = used[k - NBANKS]
            g.tensor.wait_ge(T.sem["v%d" % oc], on)
        bank = (k % NBANKS) * BANK
        prod = T.ps[:, bank:bank + (b - a)]
        g.tensor.matmul_mx(prod, T.qw[:], T.sw[:], T.qx[:, j * NC + a:j * NC + b], T.sx[:, j * NC + a:j * NC + b],
                           True, True).then_inc(T.sem["m%d" % k], 1)
        g.vector.wait_ge(T.sem["m%d" % k], 1)
        if done[c] == 0:
            g.vector.tensor_copy(T.acc[:, a:b], prod).then_inc(T.sem["v%d" % c], 1)
        else:
            g.vector.wait_ge(T.sem["v%d" % c], done[c])
            g.vector.tensor_tensor(T.acc[:, a:b], prod, T.acc[:, a:b], AluOpType.max).then_inc(T.sem["v%d" % c], 1)
        done[c] += 1
        used.append((c, done[c]))

    for c, (a, b) in enumerate(MCH):
        q = g.sync if c % 2 == 0 else g.scalar
        q.wait_ge(T.sem["v%d" % c], N)
        q.dma_start(T.y[:, a:b], T.acc[:, a:b]).then_inc(T.sem["st%d" % c], 16)
    for c in range(len(MCH)):
        q = g.sync if c % 2 == 0 else g.scalar
        q.wait_ge(T.sem["st%d" % c], 16)

    g.wait_ge(T.sem.sent, sent)
